import numpy as np
import ml_dtypes


def mxq(x, axis, fmt="e4m3"):
    dtype, down = {"e4m3": (ml_dtypes.float8_e4m3fn, 7), "e5m2": (ml_dtypes.float8_e5m2, 14)}[fmt]
    v = np.moveaxis(np.asarray(x, np.float32).astype(ml_dtypes.bfloat16).astype(np.float64), axis, -1)
    blocks = v.reshape(v.shape[:-1] + (-1, 32))
    amax = np.abs(blocks).max(-1, keepdims=True)
    byte = np.maximum(np.where(amax > 0, np.frexp(amax)[1] - 1 + 127, 0) - down, 1)
    scale = np.exp2(byte - 127.0)
    codes = (blocks / scale).astype(np.float32).astype(dtype).astype(np.float64)
    return np.moveaxis((codes * scale).reshape(v.shape), -1, axis)


WIDE = False


def mx_kscale(k):
    if not WIDE:
        return np.ones(k)
    levels = np.array([10, -10, 5, -5, 0])
    if k % 512:
        return np.exp2(np.random.permutation(np.resize(levels, k // 32))).repeat(32)
    a = np.empty((k // 512, 16))
    for p in range(k // 512):
        a[p, :8] = np.random.permutation(np.resize(levels, 8))
        for g in range(8):
            far = levels[np.abs(levels - a[p, g]) >= 10]
            a[p, g + 8] = far[np.random.randint(len(far))]
    return np.exp2(a.ravel()).repeat(32)


def f64(x):
    return np.asarray(x).astype(np.float64)


def striped(idx):
    return np.tile(idx.reshape(-1, 16).T, (8, 1)).astype(np.uint16)


def unstriped(offs):
    return offs[:16].T.reshape(-1).astype(np.int64)


def striped8(idx):
    return np.concatenate([x.reshape(-1, 16).T for x in idx]).astype(np.uint16)


def runs(offs, k):
    lists = np.stack([offs[16 * r : 16 * r + 16].T.reshape(-1) for r in range(8)]).astype(np.int64)
    return lists[np.arange(k) % 512 // 64]


def pack_weight(w):
    k, n = w.shape
    w = f64(np.asarray(w, np.float32).astype(ml_dtypes.bfloat16)).reshape(k // 32, 32, n)
    amax = np.abs(w).max(1)
    byte = np.clip(np.where(amax > 0, np.frexp(amax)[1] - 1 + 127 - 7, 1), 1, 254)
    scaled = (w * np.exp2(127.0 - byte)[:, None, :]).reshape(k, n).astype(np.float32)
    words = np.ascontiguousarray(scaled.reshape(k // 512, 128, 4, n).transpose(0, 1, 3, 2)).astype(ml_dtypes.float8_e4m3fn).view(np.uint8)
    return words, np.ascontiguousarray(byte.astype(np.uint8).reshape(k // 512, 16, n))


def unpack_weight(words, scales):
    g, p, n, _ = words.shape
    vals = np.ascontiguousarray(words).view(ml_dtypes.float8_e4m3fn).astype(np.float64) * np.repeat(np.exp2(scales.astype(np.float64) - 127.0), 8, axis=1)[..., None]
    return vals.transpose(0, 1, 3, 2).reshape(g * 512, n)


def sigmoid(v):
    return 1.0 / (1.0 + np.exp(-np.maximum(v, -700.0)))

def planes(y):
    n, m = y.shape
    v = y.astype(np.float32).astype(ml_dtypes.bfloat16).astype(np.float64).reshape(n // 32, 32, m)
    top = np.abs(v).max(1)
    byte = np.clip(np.where(top > 0, np.frexp(top)[1] - 1 + 127 - 7, 1), 1, 254)
    codes = (v * np.exp2(127.0 - byte)[:, None, :]).reshape(n, m).astype(np.float32).astype(ml_dtypes.float8_e4m3fn).view(np.uint8)
    words = codes.reshape(n // 512, 128, 4, m).transpose(0, 1, 3, 2)
    return np.ascontiguousarray(words), np.ascontiguousarray(byte.astype(np.uint8).reshape(n // 512, 16, m))


K, T, S, G, H = 512, 2048, 256, 2048, 512


def setup_inputs():
    n = np.random.standard_normal
    s = mx_kscale(K)[:, None]
    packed_xT = pack_weight(n((K, T)) * s)
    packed_dT = pack_weight(n((K, G)) / s)
    return {
        "x_words": packed_xT[0],
        "x_scales": packed_xT[1],
        "d_words": packed_dT[0],
        "d_scales": packed_dT[1],
        "sl": np.random.uniform(1.0, 2.0, (H, 1)).astype(np.float32),
        "th": (0.5 * n((H, 1))).astype(np.float32),
        "sl2": np.random.uniform(1.0, 2.0, (H, 1)).astype(np.float32),
        "th2": (0.5 * n((H, 1))).astype(np.float32),
        "gs": (np.random.uniform(0.5, 1.5, (K, 1)) * s).astype(np.float32),
        "sl3": np.random.uniform(1.0, 2.0, (H, 1)).astype(np.float32),
        "th3": (0.5 * n((H, 1))).astype(np.float32),
        "offs": striped(np.random.permutation(T)[:S]),
        "k1": striped8(np.random.randint(0, G, (8, H))),
        "n1": striped8(np.stack([np.random.permutation(S) for _ in range(8)])),
        "n2": striped8(np.stack([np.random.permutation(S) for _ in range(8)])),
        "n3": striped(np.random.permutation(S)),
        "n4": striped(np.random.permutation(S)),
    }


def reference(x_words, x_scales, d_words, d_scales, sl, th, sl2, th2, gs, sl3, th3, offs, k1, n1, n2, n3, n4):
    d_k1 = unpack_weight(d_words, d_scales)[np.arange(K)[:, None], runs(k1, K)]
    xq = unpack_weight(x_words, x_scales)[:, unstriped(offs)]
    h = 0.0625 * (d_k1.T @ xq)
    sg = sigmoid(f64(sl) * (h[np.arange(H)[:, None], runs(n1, H)] - f64(th)))
    sg2 = sigmoid(f64(sl2) * (f64(th2) - (h[np.arange(H)[:, None], runs(n2, H)])))
    z = f64(gs) * (2.0 * ((h * sg) * sg2))
    h2 = 0.0625 * ((d_k1.T @ mxq(z, 0, "e4m3")))
    sg3 = sigmoid(f64(sl3) * (h2[:, unstriped(n3)] - f64(th3)))
    st = h2 * sg3
    out_0 = st - (0.5 * st[:, unstriped(n4)])
    return (out_0,) + planes(out_0)

@@ -1,0 +1,219 @@
+from contextlib import ExitStack
+
+import concourse.mybir as mybir
+
+K, T, S, G, H = 512, 2048, 256, 2048, 512
+FLOPS = 2 * (2 * K * H * S)
+
+F32 = mybir.dt.float32
+BF16 = mybir.dt.bfloat16
+I32 = mybir.dt.int32
+U32 = mybir.dt.uint32
+U16 = mybir.dt.uint16
+U8 = mybir.dt.uint8
+FP8X4 = mybir.dt.float8_e4m3fn_x4
+MULT = mybir.AluOpType.mult
+ADD = mybir.AluOpType.add
+COPY = mybir.ActivationFunctionType.Copy
+SIGMOID = mybir.ActivationFunctionType.Sigmoid
+
+P = 128
+PACK = 4
+HALF = S // 2
+HALVES = (slice(0, HALF), slice(HALF, S))
+LIST_HALVES = (slice(0, HALF // 16), slice(HALF // 16, S // 16))
+SIGMOID_WINDOW = 2 * S
+LINE = 4
+
+
+def tile_picked_ringecrehp_none_po_kernel(
+    tc, x_words, x_scales, d_words, d_scales, sl, th, sl2, th2, gs, sl3, th3, offs, k1, n1, n2, n3, n4, out_0, out_1, out_2
+):
+    nc = tc.nc
+    with ExitStack() as ctx:
+        lists = ctx.enter_context(tc.tile_pool(name="lists", bufs=1))
+        keep = ctx.enter_context(tc.tile_pool(name="keep", bufs=1))
+        psum = ctx.enter_context(tc.psum_pool(name="psum", bufs=1))
+
+        def load_list(source, name):
+            tile = lists.tile(list(source.shape), U16, name=name)
+            nc.sync.dma_start(tile[:], source)
+            return tile
+
+        def load_words(source, name):
+            tile = keep.tile([P, source.shape[2]], I32, name=name, align_bytes=64)
+            nc.sync.dma_start(tile[:], source[0].rearrange("p c r -> p (c r)").bitcast(I32))
+            return tile
+
+        def load_scale_rows(source, name, clearing_engine):
+            tile = keep.tile([P, source.shape[2]], U8, name=name, align_bytes=64)
+            clearing_engine.memset(tile[:].bitcast(I32), 0)
+            nc.scalar.dma_start(tile[0:P:8, :].bitcast(I32), source[0].bitcast(I32))
+            return tile
+
+        def load_rows(source, name, queue):
+            tile = keep.tile([P, PACK], F32, name=name)
+            queue.dma_start(tile[:], source.rearrange("(p t) o -> p (t o)", t=PACK))
+            return tile
+
+        d_scale_table = load_scale_rows(d_scales, "d_scale_table", nc.vector)
+        x_scale_table = load_scale_rows(x_scales, "x_scale_table", nc.vector)
+        k1_list = load_list(k1, "k1_list")
+        offs_list = load_list(offs, "offs_list")
+        sl_t = load_rows(sl, "sl_t", nc.sync)
+        th_t = load_rows(th, "th_t", nc.sync)
+        d_word_table = load_words(d_words, "d_word_table")
+        n1_list = load_list(n1, "n1_list")
+        x_word_table = load_words(x_words, "x_word_table")
+        n2_list = load_list(n2, "n2_list")
+        n3_list = load_list(n3, "n3_list")
+        n4_list = load_list(n4, "n4_list")
+        sl2_t = load_rows(sl2, "sl2_t", nc.gpsimd)
+        th2_t = load_rows(th2, "th2_t", nc.gpsimd)
+        gs_t = load_rows(gs, "gs_t", nc.gpsimd)
+        sl3_t = load_rows(sl3, "sl3_t", nc.gpsimd)
+        th3_t = load_rows(th3, "th3_t", nc.gpsimd)
+
+        h_rows = [keep.tile([P, SIGMOID_WINDOW], F32, name="h_rows%d" % t, align_bytes=64) for t in range(PACK)]
+        st_rows = [keep.tile([P, S], F32, name="st_rows%d" % t, align_bytes=64) for t in range(PACK)]
+        for t in range(PACK):
+            nc.vector.memset(h_rows[t][:, S:], 0.0)
+
+        picked_scales = keep.tile([P, H + S], U8, align_bytes=64)
+        nc.vector.tensor_copy(picked_scales[:, :H], d_scale_table[:].indirect(k1_list[:]))
+        nc.vector.tensor_copy(picked_scales[:, H:], x_scale_table[:].indirect(offs_list[:]))
+        scales = keep.tile([P, H + S], U8, align_bytes=64)
+        nc.vector.tensor_copy(
+            scales[:, :H].rearrange("p (t m) -> p m t", t=PACK),
+            picked_scales[:, :H].rearrange("p (m t) -> p m t", t=PACK),
+        )
+        nc.vector.tensor_copy(scales[:, H:].bitcast(I32), picked_scales[:, H:].bitcast(I32))
+        for j in range(1, 4):
+            nc.scalar.dma_start(scales[j:P:32, :].bitcast(I32), scales[8 * j : P : 32, :].bitcast(I32))
+
+        d_picked = keep.tile([P, H], U32, align_bytes=64, tag="d_picked")
+        nc.vector.tensor_copy(d_picked[:], d_word_table[:].bitcast(U32).indirect(k1_list[:]))
+        d_dealt = keep.tile([P, H], I32, align_bytes=64)
+        nc.vector.tensor_copy(
+            d_dealt[:].rearrange("p (t m) -> p m t", t=PACK),
+            d_picked[:].bitcast(I32).rearrange("p (m t) -> p m t", t=PACK),
+        )
+        x_picked = keep.tile([P, S], U32, align_bytes=64, tag="x_picked")
+        nc.vector.tensor_copy(x_picked[:], x_word_table[:].bitcast(U32).indirect(offs_list[:]))
+
+        def product(out, t, codes, code_scales):
+            cols = slice(t * P, (t + 1) * P)
+            nc.tensor.matmul_mx(
+                out=out,
+                lhsT=d_dealt[:, cols].bitcast(FP8X4),
+                lhsT_scale=scales[:, cols],
+                rhs=codes.bitcast(FP8X4),
+                rhs_scale=code_scales,
+                start=True,
+                stop=True,
+            )
+
+        bias1 = keep.tile([P, PACK], F32)
+        nc.vector.scalar_tensor_tensor(bias1[:], sl_t[:], -1.0, th_t[:], MULT, MULT)
+        second = keep.tile([P, 3, PACK], F32, align_bytes=64, tag="d_picked")
+        scale2, bias2, gain = second[:, 0, :], second[:, 1, :], second[:, 2, :]
+        nc.vector.tensor_scalar(scale2, sl2_t[:], -1.0, None, MULT)
+        nc.vector.tensor_tensor(bias2, sl2_t[:], th2_t[:], MULT)
+        nc.vector.tensor_scalar(gain, gs_t[:], 2.0 * 0.0625, None, MULT)
+
+        first = [psum.tile([P, S], F32, name="first%d" % t, tag="bank%d" % t) for t in range(PACK)]
+        for t in range(PACK):
+            product(first[t][:], t, x_picked[:], scales[:, H:])
+        for t in range(PACK):
+            nc.vector.tensor_scalar(h_rows[t][:, :S], first[t][:], 0.0625, None, MULT)
+        sg = keep.tile([P, PACK, S], F32, align_bytes=64)
+        sg2 = keep.tile([P, PACK, S], F32, align_bytes=64)
+        gated = keep.tile([P, PACK, S], F32, align_bytes=64)
+        whole = (slice(0, S), slice(0, S // 16))
+        left = (HALVES[0], LIST_HALVES[0])
+        right = (HALVES[1], LIST_HALVES[1])
+
+        def fetch_sg(t, piece):
+            cols, entries = piece
+            col = slice(t, t + 1)
+            nc.scalar.activation(
+                sg[:, t, cols], h_rows[t][:].indirect(n1_list[:, entries]), SIGMOID, bias=bias1[:, col], scale=sl_t[:, col]
+            )
+            nc.vector.scalar_tensor_tensor(gated[:, t, cols], first[t][:, cols], gain[:, col], sg[:, t, cols], MULT, MULT)
+
+        def fetch_sg2(t, piece):
+            cols, entries = piece
+            col = slice(t, t + 1)
+            nc.scalar.activation(
+                sg2[:, t, cols], h_rows[t][:].indirect(n2_list[:, entries]), SIGMOID, bias=bias2[:, col], scale=scale2[:, col]
+            )
+
+        def by_lines(ap):
+            return ap.rearrange("p t (c i) -> p c t i", i=LINE)
+
+        def interleaved(tile):
+            return tile[:].rearrange("p (c i t) -> p c t i", i=LINE, t=PACK)
+
+        def quantised_z(half):
+            cols = HALVES[half]
+            z = keep.tile([P, HALF * PACK], BF16, name="z%d" % half, align_bytes=64, tag="rounded")
+            nc.vector.tensor_tensor(interleaved(z), by_lines(gated[:, :, cols]), by_lines(sg2[:, :, cols]), MULT)
+            z_codes = keep.tile([P, HALF], U32, name="z_codes%d" % half, align_bytes=64)
+            z_scales = keep.tile([P, HALF], U8, name="z_scales%d" % half, align_bytes=64)
+            nc.vector.quantize_mx(out=z_codes[:].bitcast(FP8X4), scales=z_scales[:], in_=z[:])
+            return z_codes[:], z_scales[:]
+
+        for t in range(2):
+            fetch_sg(t, whole)
+            fetch_sg2(t, whole)
+        fetch_sg(2, whole)
+        fetch_sg(3, left)
+        fetch_sg2(2, left)
+        fetch_sg2(3, left)
+        early = psum.tile([P, PACK, HALF], F32, name="early", tag="bank4")
+        z_left = quantised_z(0)
+        for t in range(PACK):
+            product(early[:, t, :], t, *z_left)
+        fetch_sg(3, right)
+        fetch_sg2(2, right)
+        fetch_sg2(3, right)
+
+        bias3 = keep.tile([P, PACK], F32, align_bytes=64, tag="x_picked")
+        nc.vector.scalar_tensor_tensor(bias3[:], sl3_t[:], -1.0, th3_t[:], MULT, MULT)
+
+        z_right = quantised_z(1)
+        late = [psum.tile([P, HALF], F32, name="late%d" % t, tag="bank%d" % t) for t in range(PACK)]
+        for t in range(PACK):
+            product(late[t][:], t, *z_right)
+        for t in range(PACK):
+            nc.scalar.activation(h_rows[t][:, HALVES[0]], early[:, t, :], COPY, scale=0.0625)
+        nc.scalar.activation(h_rows[0][:, HALVES[1]], late[0][:], COPY, scale=0.0625)
+        for t in range(1, PACK):
+            nc.vector.tensor_scalar(h_rows[t][:, HALVES[1]], late[t][:], 0.0625, None, MULT)
+
+        sg3 = keep.tile([P, PACK, S], F32, align_bytes=64)
+        for t in range(PACK):
+            col = slice(t, t + 1)
+            nc.scalar.activation(
+                sg3[:, t, :], h_rows[t][:].indirect(n3_list[:]), SIGMOID, bias=bias3[:, col], scale=sl3_t[:, col]
+            )
+            nc.vector.tensor_tensor(st_rows[t][:, :S], h_rows[t][:, :S], sg3[:, t, :], MULT)
+
+        fetched = keep.tile([P, PACK, S], F32, align_bytes=64)
+        result = keep.tile([P, PACK, S], F32, align_bytes=64)
+        out_rows = out_0.rearrange("(p t) c -> p t c", t=PACK)
+        y_codes = keep.tile([P, S], I32, align_bytes=64)
+        y_scales = keep.tile([P, S], U8, align_bytes=64)
+        words_out = out_1[0].rearrange("p c r -> p (c r)").bitcast(I32)
+        for half, (cols, entries) in enumerate((left, right)):
+            for t in range(PACK):
+                nc.scalar.activation(fetched[:, t, cols], st_rows[t][:].indirect(n4_list[:, entries]), COPY)
+                nc.vector.scalar_tensor_tensor(result[:, t, cols], fetched[:, t, cols], -0.5, st_rows[t][:, cols], MULT, ADD)
+            (nc.sync, nc.scalar)[half].dma_start(out_rows[:, :, cols], result[:, :, cols])
+            y = keep.tile([P, HALF * PACK], BF16, name="y%d" % half, align_bytes=64, tag="rounded")
+            nc.vector.tensor_copy(interleaved(y), by_lines(result[:, :, cols]))
+            nc.vector.quantize_mx(out=y_codes[:, cols].bitcast(FP8X4), scales=y_scales[:, cols], in_=y[:])
+            nc.sync.dma_start(words_out[:, cols], y_codes[:, cols])
+        for q in range(4):
+            queue = nc.scalar if q % 2 == 0 else nc.sync
+            queue.dma_start(out_2[0, 4 * q : 4 * q + 4, :].bitcast(I32), y_scales[32 * q : 32 * q + 4, :].bitcast(I32))

@@ -41,14 +41,14 @@ def tile_picked_ringecrehp_none_po_kernel(
             return tile
 
         def load_words(source, name):
-            tile = keep.tile([P, source.shape[2]], I32, name=name, align_bytes=64)
+            tile = keep.tile([P, source.shape[2]], I32, name=name, tag=name, align_bytes=64)
             nc.sync.dma_start(tile[:], source[0].rearrange("p c r -> p (c r)").bitcast(I32))
             return tile
 
         def load_scale_rows(source, name, clearing_engine):
             tile = keep.tile([P, source.shape[2]], U8, name=name, align_bytes=64)
             clearing_engine.memset(tile[:].bitcast(I32), 0)
-            nc.scalar.dma_start(tile[0:P:8, :].bitcast(I32), source[0].bitcast(I32))
+            nc.sync.dma_start(tile[0:P:8, :].bitcast(I32), source[0].bitcast(I32))
             return tile
 
         def load_rows(source, name, queue):
@@ -91,14 +91,14 @@ def tile_picked_ringecrehp_none_po_kernel(
         for j in range(1, 4):
             nc.scalar.dma_start(scales[j:P:32, :].bitcast(I32), scales[8 * j : P : 32, :].bitcast(I32))
 
-        d_picked = keep.tile([P, H], U32, align_bytes=64, tag="d_picked")
+        d_picked = keep.tile([P, H], U32, align_bytes=64)
         nc.vector.tensor_copy(d_picked[:], d_word_table[:].bitcast(U32).indirect(k1_list[:]))
         d_dealt = keep.tile([P, H], I32, align_bytes=64)
         nc.vector.tensor_copy(
             d_dealt[:].rearrange("p (t m) -> p m t", t=PACK),
             d_picked[:].bitcast(I32).rearrange("p (m t) -> p m t", t=PACK),
         )
-        x_picked = keep.tile([P, S], U32, align_bytes=64, tag="x_picked")
+        x_picked = keep.tile([P, S], U32, align_bytes=64)
         nc.vector.tensor_copy(x_picked[:], x_word_table[:].bitcast(U32).indirect(offs_list[:]))
 
         def product(out, t, codes, code_scales):
@@ -115,7 +115,7 @@ def tile_picked_ringecrehp_none_po_kernel(
 
         bias1 = keep.tile([P, PACK], F32)
         nc.vector.scalar_tensor_tensor(bias1[:], sl_t[:], -1.0, th_t[:], MULT, MULT)
-        second = keep.tile([P, 3, PACK], F32, align_bytes=64, tag="d_picked")
+        second = keep.tile([P, 3, PACK], F32, align_bytes=64, tag="x_word_table")
         scale2, bias2, gain = second[:, 0, :], second[:, 1, :], second[:, 2, :]
         nc.vector.tensor_scalar(scale2, sl2_t[:], -1.0, None, MULT)
         nc.vector.tensor_tensor(bias2, sl2_t[:], th2_t[:], MULT)
@@ -126,92 +126,70 @@ def tile_picked_ringecrehp_none_po_kernel(
             product(first[t][:], t, x_picked[:], scales[:, H:])
         for t in range(PACK):
             nc.vector.tensor_scalar(h_rows[t][:, :S], first[t][:], 0.0625, None, MULT)
-        sg = keep.tile([P, PACK, S], F32, align_bytes=64)
-        sg2 = keep.tile([P, PACK, S], F32, align_bytes=64)
-        gated = keep.tile([P, PACK, S], F32, align_bytes=64)
-        whole = (slice(0, S), slice(0, S // 16))
-        left = (HALVES[0], LIST_HALVES[0])
-        right = (HALVES[1], LIST_HALVES[1])
-
-        def fetch_sg(t, piece):
-            cols, entries = piece
-            col = slice(t, t + 1)
-            nc.scalar.activation(
-                sg[:, t, cols], h_rows[t][:].indirect(n1_list[:, entries]), SIGMOID, bias=bias1[:, col], scale=sl_t[:, col]
-            )
-            nc.vector.scalar_tensor_tensor(gated[:, t, cols], first[t][:, cols], gain[:, col], sg[:, t, cols], MULT, MULT)
-
-        def fetch_sg2(t, piece):
-            cols, entries = piece
-            col = slice(t, t + 1)
-            nc.scalar.activation(
-                sg2[:, t, cols], h_rows[t][:].indirect(n2_list[:, entries]), SIGMOID, bias=bias2[:, col], scale=scale2[:, col]
-            )
-
-        def by_lines(ap):
-            return ap.rearrange("p t (c i) -> p c t i", i=LINE)
+        def by_lines(tile):
+            return tile[:].rearrange("p t (c i) -> p c t i", i=LINE)
 
         def interleaved(tile):
             return tile[:].rearrange("p (c i t) -> p c t i", i=LINE, t=PACK)
 
-        def quantised_z(half):
-            cols = HALVES[half]
+        early = psum.tile([P, PACK, HALF], F32, name="early", tag="bank4")
+        second_sums = [[early[:, t, :] for t in range(PACK)]]
+        for half in range(2):
+            cols, entries = HALVES[half], LIST_HALVES[half]
+            gated = keep.tile([P, PACK, HALF], F32, name="gated%d" % half, tag="gated%d" % half, align_bytes=64)
+            sg2 = keep.tile([P, PACK, HALF], F32, name="sg2_%d" % half, align_bytes=64, tag="sg2")
+            for t in range(PACK):
+                col = slice(t, t + 1)
+                sg = keep.tile([P, HALF], F32, name="sg", align_bytes=64, bufs=3)
+                nc.scalar.activation(
+                    sg[:], h_rows[t][:].indirect(n1_list[:, entries]), SIGMOID, bias=bias1[:, col], scale=sl_t[:, col]
+                )
+                nc.scalar.activation(
+                    sg2[:, t, :], h_rows[t][:].indirect(n2_list[:, entries]), SIGMOID, bias=bias2[:, col], scale=scale2[:, col]
+                )
+                nc.vector.scalar_tensor_tensor(gated[:, t, :], first[t][:, cols], gain[:, col], sg[:], MULT, MULT)
             z = keep.tile([P, HALF * PACK], BF16, name="z%d" % half, align_bytes=64, tag="rounded")
-            nc.vector.tensor_tensor(interleaved(z), by_lines(gated[:, :, cols]), by_lines(sg2[:, :, cols]), MULT)
+            nc.vector.tensor_tensor(interleaved(z), by_lines(gated), by_lines(sg2), MULT)
             z_codes = keep.tile([P, HALF], U32, name="z_codes%d" % half, align_bytes=64)
             z_scales = keep.tile([P, HALF], U8, name="z_scales%d" % half, align_bytes=64)
             nc.vector.quantize_mx(out=z_codes[:].bitcast(FP8X4), scales=z_scales[:], in_=z[:])
-            return z_codes[:], z_scales[:]
+            if half == 1:
+                second_sums.append(
+                    [psum.tile([P, HALF], F32, name="late%d" % t, tag="bank%d" % t)[:] for t in range(PACK)]
+                )
+            for t in range(PACK):
+                product(second_sums[half][t], t, z_codes[:], z_scales[:])
 
-        for t in range(2):
-            fetch_sg(t, whole)
-            fetch_sg2(t, whole)
-        fetch_sg(2, whole)
-        fetch_sg(3, left)
-        fetch_sg2(2, left)
-        fetch_sg2(3, left)
-        early = psum.tile([P, PACK, HALF], F32, name="early", tag="bank4")
-        z_left = quantised_z(0)
         for t in range(PACK):
-            product(early[:, t, :], t, *z_left)
-        fetch_sg(3, right)
-        fetch_sg2(2, right)
-        fetch_sg2(3, right)
-
-        bias3 = keep.tile([P, PACK], F32, align_bytes=64, tag="x_picked")
-        nc.vector.scalar_tensor_tensor(bias3[:], sl3_t[:], -1.0, th3_t[:], MULT, MULT)
-
-        z_right = quantised_z(1)
-        late = [psum.tile([P, HALF], F32, name="late%d" % t, tag="bank%d" % t) for t in range(PACK)]
-        for t in range(PACK):
-            product(late[t][:], t, *z_right)
-        for t in range(PACK):
-            nc.scalar.activation(h_rows[t][:, HALVES[0]], early[:, t, :], COPY, scale=0.0625)
-        nc.scalar.activation(h_rows[0][:, HALVES[1]], late[0][:], COPY, scale=0.0625)
+            nc.scalar.activation(h_rows[t][:, HALVES[0]], second_sums[0][t], COPY, scale=0.0625)
+        nc.scalar.activation(h_rows[0][:, HALVES[1]], second_sums[1][0], COPY, scale=0.0625)
         for t in range(1, PACK):
-            nc.vector.tensor_scalar(h_rows[t][:, HALVES[1]], late[t][:], 0.0625, None, MULT)
+            nc.vector.tensor_scalar(h_rows[t][:, HALVES[1]], second_sums[1][t], 0.0625, None, MULT)
 
+        bias3 = keep.tile([P, PACK], F32, align_bytes=64, tag="gated0")
+        nc.vector.scalar_tensor_tensor(bias3[:], sl3_t[:], -1.0, th3_t[:], MULT, MULT)
         sg3 = keep.tile([P, PACK, S], F32, align_bytes=64)
         for t in range(PACK):
             col = slice(t, t + 1)
             nc.scalar.activation(
                 sg3[:, t, :], h_rows[t][:].indirect(n3_list[:]), SIGMOID, bias=bias3[:, col], scale=sl3_t[:, col]
             )
-            nc.vector.tensor_tensor(st_rows[t][:, :S], h_rows[t][:, :S], sg3[:, t, :], MULT)
+            nc.vector.tensor_tensor(st_rows[t][:], h_rows[t][:, :S], sg3[:, t, :], MULT)
 
-        fetched = keep.tile([P, PACK, S], F32, align_bytes=64)
-        result = keep.tile([P, PACK, S], F32, align_bytes=64)
         out_rows = out_0.rearrange("(p t) c -> p t c", t=PACK)
         y_codes = keep.tile([P, S], I32, align_bytes=64)
         y_scales = keep.tile([P, S], U8, align_bytes=64)
         words_out = out_1[0].rearrange("p c r -> p (c r)").bitcast(I32)
-        for half, (cols, entries) in enumerate((left, right)):
+        for half in range(2):
+            cols, entries = HALVES[half], LIST_HALVES[half]
+            result = keep.tile([P, PACK, HALF], F32, name="result%d" % half, align_bytes=64)
             for t in range(PACK):
-                nc.scalar.activation(fetched[:, t, cols], st_rows[t][:].indirect(n4_list[:, entries]), COPY)
-                nc.vector.scalar_tensor_tensor(result[:, t, cols], fetched[:, t, cols], -0.5, st_rows[t][:, cols], MULT, ADD)
-            (nc.sync, nc.scalar)[half].dma_start(out_rows[:, :, cols], result[:, :, cols])
+                fetched = keep.tile([P, HALF], F32, name="fetched", align_bytes=64, bufs=3)
+                nc.scalar.activation(fetched[:], st_rows[t][:].indirect(n4_list[:, entries]), COPY)
+                nc.vector.scalar_tensor_tensor(result[:, t, :], fetched[:], -0.5, st_rows[t][:, cols], MULT, ADD)
+            (nc.sync, nc.scalar)[half].dma_start(out_rows[:, :, cols], result[:])
             y = keep.tile([P, HALF * PACK], BF16, name="y%d" % half, align_bytes=64, tag="rounded")
-            nc.vector.tensor_copy(interleaved(y), by_lines(result[:, :, cols]))
+            nc.vector.tensor_copy(interleaved(y), by_lines(result))
             nc.vector.quantize_mx(out=y_codes[:, cols].bitcast(FP8X4), scales=y_scales[:, cols], in_=y[:])
             nc.sync.dma_start(words_out[:, cols], y_codes[:, cols])
         for q in range(4):

@@ -45,9 +45,12 @@ def tile_picked_ringecrehp_none_po_kernel(
             nc.sync.dma_start(tile[:], source[0].rearrange("p c r -> p (c r)").bitcast(I32))
             return tile
 
-        def load_scale_rows(source, name, clearing_engine):
-            tile = keep.tile([P, source.shape[2]], U8, name=name, align_bytes=64)
-            clearing_engine.memset(tile[:].bitcast(I32), 0)
+        def load_scale_rows(source, name, cleared_by_vector):
+            width = source.shape[2]
+            tile = keep.tile([P, width], U8, name=name, align_bytes=64)
+            nc.vector.memset(tile[:, :cleared_by_vector].bitcast(I32), 0)
+            if cleared_by_vector < width:
+                nc.gpsimd.memset(tile[:, cleared_by_vector:].bitcast(I32), 0)
             nc.sync.dma_start(tile[0:P:8, :].bitcast(I32), source[0].bitcast(I32))
             return tile
 
@@ -56,8 +59,8 @@ def tile_picked_ringecrehp_none_po_kernel(
             queue.dma_start(tile[:], source.rearrange("(p t) o -> p (t o)", t=PACK))
             return tile
 
-        d_scale_table = load_scale_rows(d_scales, "d_scale_table", nc.vector)
-        x_scale_table = load_scale_rows(x_scales, "x_scale_table", nc.vector)
+        d_scale_table = load_scale_rows(d_scales, "d_scale_table", G)
+        x_scale_table = load_scale_rows(x_scales, "x_scale_table", T // 2)
         k1_list = load_list(k1, "k1_list")
         offs_list = load_list(offs, "offs_list")
         sl_t = load_rows(sl, "sl_t", nc.sync)
@@ -99,7 +102,10 @@ def tile_picked_ringecrehp_none_po_kernel(
             d_picked[:].bitcast(I32).rearrange("p (m t) -> p m t", t=PACK),
         )
         x_picked = keep.tile([P, S], U32, align_bytes=64)
-        nc.vector.tensor_copy(x_picked[:], x_word_table[:].bitcast(U32).indirect(offs_list[:]))
+        for half in range(2):
+            nc.vector.tensor_copy(
+                x_picked[:, HALVES[half]], x_word_table[:].bitcast(U32).indirect(offs_list[:, LIST_HALVES[half]])
+            )
 
         def product(out, t, codes, code_scales):
             cols = slice(t * P, (t + 1) * P)
@@ -119,37 +125,60 @@ def tile_picked_ringecrehp_none_po_kernel(
         scale2, bias2, gain = second[:, 0, :], second[:, 1, :], second[:, 2, :]
         nc.vector.tensor_scalar(scale2, sl2_t[:], -1.0, None, MULT)
         nc.vector.tensor_tensor(bias2, sl2_t[:], th2_t[:], MULT)
-        nc.vector.tensor_scalar(gain, gs_t[:], 2.0 * 0.0625, None, MULT)
+        nc.vector.tensor_scalar(gain, gs_t[:], 2.0, None, MULT)
 
-        first = [psum.tile([P, S], F32, name="first%d" % t, tag="bank%d" % t) for t in range(PACK)]
-        for t in range(PACK):
-            product(first[t][:], t, x_picked[:], scales[:, H:])
-        for t in range(PACK):
-            nc.vector.tensor_scalar(h_rows[t][:, :S], first[t][:], 0.0625, None, MULT)
-        def by_lines(tile):
-            return tile[:].rearrange("p t (c i) -> p c t i", i=LINE)
+        x_picked_scales = scales[:, H:]
+        first_pieces = [(0, HALVES[0]), (0, HALVES[1])] + [(t, slice(0, S)) for t in range(1, PACK)]
+        for bank, (t, cols) in enumerate(first_pieces):
+            sums = psum.tile([P, cols.stop - cols.start], F32, name="first%d" % bank, tag="bank%d" % bank)
+            product(sums[:], t, x_picked[:, cols], x_picked_scales[:, cols])
+            nc.vector.tensor_scalar(h_rows[t][:, cols], sums[:], 0.0625, None, MULT)
+
+        def by_lines(ap):
+            return ap.rearrange("p t (c i) -> p c t i", i=LINE)
 
         def interleaved(tile):
             return tile[:].rearrange("p (c i t) -> p c t i", i=LINE, t=PACK)
 
-        early = psum.tile([P, PACK, HALF], F32, name="early", tag="bank4")
+        gated = keep.tile([P, 2, PACK, HALF], F32, align_bytes=64, tag="gated")
+
+        def fetch_sg(t):
+            col = slice(t, t + 1)
+            sg = keep.tile([P, S], F32, name="sg%d" % t, tag="sg%d" % t, align_bytes=64)
+            nc.scalar.activation(sg[:], h_rows[t][:].indirect(n1_list[:]), SIGMOID, bias=bias1[:, col], scale=sl_t[:, col])
+            nc.vector.scalar_tensor_tensor(
+                gated[:, :, t, :],
+                h_rows[t][:, :S].rearrange("p (h c) -> p h c", h=2),
+                gain[:, col],
+                sg[:].rearrange("p (h c) -> p h c", h=2),
+                MULT,
+                MULT,
+            )
+
+        def fetch_sg2(sg2, t, half):
+            col = slice(t, t + 1)
+            nc.scalar.activation(
+                sg2[:, t, :], h_rows[t][:].indirect(n2_list[:, LIST_HALVES[half]]), SIGMOID, bias=bias2[:, col], scale=scale2[:, col]
+            )
+
+        early = psum.tile([P, PACK, HALF], F32, name="early", tag="bank5")
         second_sums = [[early[:, t, :] for t in range(PACK)]]
         for half in range(2):
-            cols, entries = HALVES[half], LIST_HALVES[half]
-            gated = keep.tile([P, PACK, HALF], F32, name="gated%d" % half, tag="gated%d" % half, align_bytes=64)
-            sg2 = keep.tile([P, PACK, HALF], F32, name="sg2_%d" % half, align_bytes=64, tag="sg2")
-            for t in range(PACK):
-                col = slice(t, t + 1)
-                sg = keep.tile([P, HALF], F32, name="sg", align_bytes=64, bufs=3)
-                nc.scalar.activation(
-                    sg[:], h_rows[t][:].indirect(n1_list[:, entries]), SIGMOID, bias=bias1[:, col], scale=sl_t[:, col]
-                )
-                nc.scalar.activation(
-                    sg2[:, t, :], h_rows[t][:].indirect(n2_list[:, entries]), SIGMOID, bias=bias2[:, col], scale=scale2[:, col]
-                )
-                nc.vector.scalar_tensor_tensor(gated[:, t, :], first[t][:, cols], gain[:, col], sg[:], MULT, MULT)
+            if half == 0:
+                sg2 = keep.tile([P, PACK, HALF], F32, name="sg2_left", align_bytes=64)
+                for t in range(2):
+                    fetch_sg(t)
+                    fetch_sg2(sg2, t, 0)
+                for t in range(2, PACK):
+                    fetch_sg(t)
+                for t in range(2, PACK):
+                    fetch_sg2(sg2, t, 0)
+            else:
+                sg2 = keep.tile([P, PACK, HALF], F32, name="sg2_right", tag="sg3", align_bytes=64)
+                for t in range(PACK):
+                    fetch_sg2(sg2, t, 1)
             z = keep.tile([P, HALF * PACK], BF16, name="z%d" % half, align_bytes=64, tag="rounded")
-            nc.vector.tensor_tensor(interleaved(z), by_lines(gated), by_lines(sg2), MULT)
+            nc.vector.tensor_tensor(interleaved(z), by_lines(gated[:, half]), by_lines(sg2[:]), MULT)
             z_codes = keep.tile([P, HALF], U32, name="z_codes%d" % half, align_bytes=64)
             z_scales = keep.tile([P, HALF], U8, name="z_scales%d" % half, align_bytes=64)
             nc.vector.quantize_mx(out=z_codes[:].bitcast(FP8X4), scales=z_scales[:], in_=z[:])
@@ -166,9 +195,9 @@ def tile_picked_ringecrehp_none_po_kernel(
         for t in range(1, PACK):
             nc.vector.tensor_scalar(h_rows[t][:, HALVES[1]], second_sums[1][t], 0.0625, None, MULT)
 
-        bias3 = keep.tile([P, PACK], F32, align_bytes=64, tag="gated0")
+        bias3 = keep.tile([P, PACK], F32, align_bytes=64, tag="sg2")
         nc.vector.scalar_tensor_tensor(bias3[:], sl3_t[:], -1.0, th3_t[:], MULT, MULT)
-        sg3 = keep.tile([P, PACK, S], F32, align_bytes=64)
+        sg3 = keep.tile([P, PACK, S], F32, align_bytes=64, tag="sg_third")
         for t in range(PACK):
             col = slice(t, t + 1)
             nc.scalar.activation(
@@ -184,12 +213,12 @@ def tile_picked_ringecrehp_none_po_kernel(
             cols, entries = HALVES[half], LIST_HALVES[half]
             result = keep.tile([P, PACK, HALF], F32, name="result%d" % half, align_bytes=64)
             for t in range(PACK):
-                fetched = keep.tile([P, HALF], F32, name="fetched", align_bytes=64, bufs=3)
+                fetched = keep.tile([P, HALF], F32, name="fetched", align_bytes=64, bufs=4)
                 nc.scalar.activation(fetched[:], st_rows[t][:].indirect(n4_list[:, entries]), COPY)
                 nc.vector.scalar_tensor_tensor(result[:, t, :], fetched[:], -0.5, st_rows[t][:, cols], MULT, ADD)
             (nc.sync, nc.scalar)[half].dma_start(out_rows[:, :, cols], result[:])
             y = keep.tile([P, HALF * PACK], BF16, name="y%d" % half, align_bytes=64, tag="rounded")
-            nc.vector.tensor_copy(interleaved(y), by_lines(result))
+            nc.vector.tensor_copy(interleaved(y), by_lines(result[:]))
             nc.vector.quantize_mx(out=y_codes[:, cols].bitcast(FP8X4), scales=y_scales[:, cols], in_=y[:])
             nc.sync.dma_start(words_out[:, cols], y_codes[:, cols])
         for q in range(4):

@@ -45,13 +45,13 @@ def tile_picked_ringecrehp_none_po_kernel(
             nc.sync.dma_start(tile[:], source[0].rearrange("p c r -> p (c r)").bitcast(I32))
             return tile
 
-        def load_scale_rows(source, name, cleared_by_vector):
+        def load_scale_rows(source, name, cleared_by_vector, queue):
             width = source.shape[2]
             tile = keep.tile([P, width], U8, name=name, align_bytes=64)
             nc.vector.memset(tile[:, :cleared_by_vector].bitcast(I32), 0)
             if cleared_by_vector < width:
                 nc.gpsimd.memset(tile[:, cleared_by_vector:].bitcast(I32), 0)
-            nc.sync.dma_start(tile[0:P:8, :].bitcast(I32), source[0].bitcast(I32))
+            queue.dma_start(tile[0:P:8, :].bitcast(I32), source[0].bitcast(I32))
             return tile
 
         def load_rows(source, name, queue):
@@ -59,14 +59,14 @@ def tile_picked_ringecrehp_none_po_kernel(
             queue.dma_start(tile[:], source.rearrange("(p t) o -> p (t o)", t=PACK))
             return tile
 
-        d_scale_table = load_scale_rows(d_scales, "d_scale_table", G)
-        x_scale_table = load_scale_rows(x_scales, "x_scale_table", T // 2)
+        d_scale_table = load_scale_rows(d_scales, "d_scale_table", G // 2, nc.sync)
+        x_scale_table = load_scale_rows(x_scales, "x_scale_table", T, nc.scalar)
         k1_list = load_list(k1, "k1_list")
         offs_list = load_list(offs, "offs_list")
-        sl_t = load_rows(sl, "sl_t", nc.sync)
-        th_t = load_rows(th, "th_t", nc.sync)
-        d_word_table = load_words(d_words, "d_word_table")
+        sl_t = load_rows(sl, "sl_t", nc.scalar)
+        th_t = load_rows(th, "th_t", nc.scalar)
         n1_list = load_list(n1, "n1_list")
+        d_word_table = load_words(d_words, "d_word_table")
         x_word_table = load_words(x_words, "x_word_table")
         n2_list = load_list(n2, "n2_list")
         n3_list = load_list(n3, "n3_list")
@@ -142,15 +142,20 @@ def tile_picked_ringecrehp_none_po_kernel(
 
         gated = keep.tile([P, 2, PACK, HALF], F32, align_bytes=64, tag="gated")
 
-        def fetch_sg(t):
+        def fetch_sg(t, halves):
             col = slice(t, t + 1)
-            sg = keep.tile([P, S], F32, name="sg%d" % t, tag="sg%d" % t, align_bytes=64)
-            nc.scalar.activation(sg[:], h_rows[t][:].indirect(n1_list[:]), SIGMOID, bias=bias1[:, col], scale=sl_t[:, col])
+            cols = slice(halves.start * HALF, halves.stop * HALF)
+            entries = slice(cols.start // 16, cols.stop // 16)
+            name = "sg%d_%d" % (t, halves.start)
+            sg = keep.tile([P, cols.stop - cols.start], F32, name=name, tag=name, align_bytes=64)
+            nc.scalar.activation(
+                sg[:], h_rows[t][:].indirect(n1_list[:, entries]), SIGMOID, bias=bias1[:, col], scale=sl_t[:, col]
+            )
             nc.vector.scalar_tensor_tensor(
-                gated[:, :, t, :],
-                h_rows[t][:, :S].rearrange("p (h c) -> p h c", h=2),
+                gated[:, halves, t, :],
+                h_rows[t][:, cols].rearrange("p (h c) -> p h c", c=HALF),
                 gain[:, col],
-                sg[:].rearrange("p (h c) -> p h c", h=2),
+                sg[:].rearrange("p (h c) -> p h c", c=HALF),
                 MULT,
                 MULT,
             )
@@ -167,14 +172,15 @@ def tile_picked_ringecrehp_none_po_kernel(
             if half == 0:
                 sg2 = keep.tile([P, PACK, HALF], F32, name="sg2_left", align_bytes=64)
                 for t in range(2):
-                    fetch_sg(t)
+                    fetch_sg(t, slice(0, 2))
                     fetch_sg2(sg2, t, 0)
-                for t in range(2, PACK):
-                    fetch_sg(t)
+                fetch_sg(2, slice(0, 2))
+                fetch_sg(3, slice(0, 1))
                 for t in range(2, PACK):
                     fetch_sg2(sg2, t, 0)
             else:
-                sg2 = keep.tile([P, PACK, HALF], F32, name="sg2_right", tag="sg3", align_bytes=64)
+                sg2 = keep.tile([P, PACK, HALF], F32, name="sg2_right", tag="sg3_0", align_bytes=64)
+                fetch_sg(3, slice(1, 2))
                 for t in range(PACK):
                     fetch_sg2(sg2, t, 1)
             z = keep.tile([P, HALF * PACK], BF16, name="z%d" % half, align_bytes=64, tag="rounded")
@@ -195,7 +201,7 @@ def tile_picked_ringecrehp_none_po_kernel(
         for t in range(1, PACK):
             nc.vector.tensor_scalar(h_rows[t][:, HALVES[1]], second_sums[1][t], 0.0625, None, MULT)
 
-        bias3 = keep.tile([P, PACK], F32, align_bytes=64, tag="sg2")
+        bias3 = keep.tile([P, PACK], F32, align_bytes=64, tag="sg2_0")
         nc.vector.scalar_tensor_tensor(bias3[:], sl3_t[:], -1.0, th3_t[:], MULT, MULT)
         sg3 = keep.tile([P, PACK, S], F32, align_bytes=64, tag="sg_third")
         for t in range(PACK):

from contextlib import ExitStack

import concourse.mybir as mybir

K, T, S, G, H = 512, 2048, 256, 2048, 512
FLOPS = 2 * (2 * K * H * S)

F32 = mybir.dt.float32
BF16 = mybir.dt.bfloat16
I32 = mybir.dt.int32
U32 = mybir.dt.uint32
U16 = mybir.dt.uint16
U8 = mybir.dt.uint8
FP8X4 = mybir.dt.float8_e4m3fn_x4
MULT = mybir.AluOpType.mult
ADD = mybir.AluOpType.add
COPY = mybir.ActivationFunctionType.Copy
SIGMOID = mybir.ActivationFunctionType.Sigmoid

P = 128
PACK = 4
HALF = S // 2
HALVES = (slice(0, HALF), slice(HALF, S))
LIST_HALVES = (slice(0, HALF // 16), slice(HALF // 16, S // 16))
SIGMOID_WINDOW = 2 * S
LINE = 4


def tile_picked_ringecrehp_none_po_kernel(
    tc, x_words, x_scales, d_words, d_scales, sl, th, sl2, th2, gs, sl3, th3, offs, k1, n1, n2, n3, n4, out_0, out_1, out_2
):
    nc = tc.nc
    with ExitStack() as ctx:
        lists = ctx.enter_context(tc.tile_pool(name="lists", bufs=1))
        keep = ctx.enter_context(tc.tile_pool(name="keep", bufs=1))
        psum = ctx.enter_context(tc.psum_pool(name="psum", bufs=1))

        def load_list(source, name):
            tile = lists.tile(list(source.shape), U16, name=name)
            nc.sync.dma_start(tile[:], source)
            return tile

        def load_words(source, name):
            tile = keep.tile([P, source.shape[2]], I32, name=name, tag=name, align_bytes=64)
            nc.sync.dma_start(tile[:], source[0].rearrange("p c r -> p (c r)").bitcast(I32))
            return tile

        def load_scale_rows(source, name, cleared_by_vector, queue):
            width = source.shape[2]
            tile = keep.tile([P, width], U8, name=name, align_bytes=64)
            nc.vector.memset(tile[:, :cleared_by_vector].bitcast(I32), 0)
            if cleared_by_vector < width:
                nc.gpsimd.memset(tile[:, cleared_by_vector:].bitcast(I32), 0)
            queue.dma_start(tile[0:P:8, :].bitcast(I32), source[0].bitcast(I32))
            return tile

        def load_rows(source, name, queue):
            tile = keep.tile([P, PACK], F32, name=name)
            queue.dma_start(tile[:], source.rearrange("(p t) o -> p (t o)", t=PACK))
            return tile

        d_scale_table = load_scale_rows(d_scales, "d_scale_table", G // 2, nc.sync)
        x_scale_table = load_scale_rows(x_scales, "x_scale_table", T, nc.scalar)
        k1_list = load_list(k1, "k1_list")
        offs_list = load_list(offs, "offs_list")
        sl_t = load_rows(sl, "sl_t", nc.scalar)
        th_t = load_rows(th, "th_t", nc.scalar)
        n1_list = load_list(n1, "n1_list")
        d_word_table = load_words(d_words, "d_word_table")
        x_word_table = load_words(x_words, "x_word_table")
        n2_list = load_list(n2, "n2_list")
        n3_list = load_list(n3, "n3_list")
        n4_list = load_list(n4, "n4_list")
        sl2_t = load_rows(sl2, "sl2_t", nc.gpsimd)
        th2_t = load_rows(th2, "th2_t", nc.gpsimd)
        gs_t = load_rows(gs, "gs_t", nc.gpsimd)
        sl3_t = load_rows(sl3, "sl3_t", nc.gpsimd)
        th3_t = load_rows(th3, "th3_t", nc.gpsimd)

        h_rows = [keep.tile([P, SIGMOID_WINDOW], F32, name="h_rows%d" % t, align_bytes=64) for t in range(PACK)]
        st_rows = [keep.tile([P, S], F32, name="st_rows%d" % t, align_bytes=64) for t in range(PACK)]
        for t in range(PACK):
            nc.vector.memset(h_rows[t][:, S:], 0.0)

        picked_scales = keep.tile([P, H + S], U8, align_bytes=64)
        nc.vector.tensor_copy(picked_scales[:, :H], d_scale_table[:].indirect(k1_list[:]))
        nc.vector.tensor_copy(picked_scales[:, H:], x_scale_table[:].indirect(offs_list[:]))
        scales = keep.tile([P, H + S], U8, align_bytes=64)
        nc.vector.tensor_copy(
            scales[:, :H].rearrange("p (t m) -> p m t", t=PACK),
            picked_scales[:, :H].rearrange("p (m t) -> p m t", t=PACK),
        )
        nc.vector.tensor_copy(scales[:, H:].bitcast(I32), picked_scales[:, H:].bitcast(I32))
        for j in range(1, 4):
            nc.scalar.dma_start(scales[j:P:32, :].bitcast(I32), scales[8 * j : P : 32, :].bitcast(I32))

        d_picked = keep.tile([P, H], U32, align_bytes=64)
        nc.vector.tensor_copy(d_picked[:], d_word_table[:].bitcast(U32).indirect(k1_list[:]))
        d_dealt = keep.tile([P, H], I32, align_bytes=64)
        nc.vector.tensor_copy(
            d_dealt[:].rearrange("p (t m) -> p m t", t=PACK),
            d_picked[:].bitcast(I32).rearrange("p (m t) -> p m t", t=PACK),
        )
        x_picked = keep.tile([P, S], U32, align_bytes=64)
        for half in range(2):
            nc.vector.tensor_copy(
                x_picked[:, HALVES[half]], x_word_table[:].bitcast(U32).indirect(offs_list[:, LIST_HALVES[half]])
            )

        def product(out, t, codes, code_scales):
            cols = slice(t * P, (t + 1) * P)
            nc.tensor.matmul_mx(
                out=out,
                lhsT=d_dealt[:, cols].bitcast(FP8X4),
                lhsT_scale=scales[:, cols],
                rhs=codes.bitcast(FP8X4),
                rhs_scale=code_scales,
                start=True,
                stop=True,
            )

        bias1 = keep.tile([P, PACK], F32)
        nc.vector.scalar_tensor_tensor(bias1[:], sl_t[:], -1.0, th_t[:], MULT, MULT)
        second = keep.tile([P, 3, PACK], F32, align_bytes=64, tag="x_word_table")
        scale2, bias2, gain = second[:, 0, :], second[:, 1, :], second[:, 2, :]
        nc.vector.tensor_scalar(scale2, sl2_t[:], -1.0, None, MULT)
        nc.vector.tensor_tensor(bias2, sl2_t[:], th2_t[:], MULT)
        nc.vector.tensor_scalar(gain, gs_t[:], 2.0, None, MULT)

        x_picked_scales = scales[:, H:]
        first_pieces = [(0, HALVES[0]), (0, HALVES[1])] + [(t, slice(0, S)) for t in range(1, PACK)]
        for bank, (t, cols) in enumerate(first_pieces):
            sums = psum.tile([P, cols.stop - cols.start], F32, name="first%d" % bank, tag="bank%d" % bank)
            product(sums[:], t, x_picked[:, cols], x_picked_scales[:, cols])
            nc.vector.tensor_scalar(h_rows[t][:, cols], sums[:], 0.0625, None, MULT)

        def by_lines(ap):
            return ap.rearrange("p t (c i) -> p c t i", i=LINE)

        def interleaved(tile):
            return tile[:].rearrange("p (c i t) -> p c t i", i=LINE, t=PACK)

        gated = keep.tile([P, 2, PACK, HALF], F32, align_bytes=64, tag="gated")

        def fetch_sg(t, halves):
            col = slice(t, t + 1)
            cols = slice(halves.start * HALF, halves.stop * HALF)
            entries = slice(cols.start // 16, cols.stop // 16)
            name = "sg%d_%d" % (t, halves.start)
            sg = keep.tile([P, cols.stop - cols.start], F32, name=name, tag=name, align_bytes=64)
            nc.scalar.activation(
                sg[:], h_rows[t][:].indirect(n1_list[:, entries]), SIGMOID, bias=bias1[:, col], scale=sl_t[:, col]
            )
            nc.vector.scalar_tensor_tensor(
                gated[:, halves, t, :],
                h_rows[t][:, cols].rearrange("p (h c) -> p h c", c=HALF),
                gain[:, col],
                sg[:].rearrange("p (h c) -> p h c", c=HALF),
                MULT,
                MULT,
            )

        def fetch_sg2(sg2, t, half):
            col = slice(t, t + 1)
            nc.scalar.activation(
                sg2[:, t, :], h_rows[t][:].indirect(n2_list[:, LIST_HALVES[half]]), SIGMOID, bias=bias2[:, col], scale=scale2[:, col]
            )

        early = psum.tile([P, PACK, HALF], F32, name="early", tag="bank5")
        second_sums = [[early[:, t, :] for t in range(PACK)]]
        for half in range(2):
            if half == 0:
                sg2 = keep.tile([P, PACK, HALF], F32, name="sg2_left", align_bytes=64)
                for t in range(2):
                    fetch_sg(t, slice(0, 2))
                    fetch_sg2(sg2, t, 0)
                fetch_sg(2, slice(0, 2))
                fetch_sg(3, slice(0, 1))
                for t in range(2, PACK):
                    fetch_sg2(sg2, t, 0)
            else:
                sg2 = keep.tile([P, PACK, HALF], F32, name="sg2_right", tag="sg3_0", align_bytes=64)
                fetch_sg(3, slice(1, 2))
                for t in range(PACK):
                    fetch_sg2(sg2, t, 1)
            z = keep.tile([P, HALF * PACK], BF16, name="z%d" % half, align_bytes=64, tag="rounded")
            nc.vector.tensor_tensor(interleaved(z), by_lines(gated[:, half]), by_lines(sg2[:]), MULT)
            z_codes = keep.tile([P, HALF], U32, name="z_codes%d" % half, align_bytes=64)
            z_scales = keep.tile([P, HALF], U8, name="z_scales%d" % half, align_bytes=64)
            nc.vector.quantize_mx(out=z_codes[:].bitcast(FP8X4), scales=z_scales[:], in_=z[:])
            if half == 1:
                second_sums.append(
                    [psum.tile([P, HALF], F32, name="late%d" % t, tag="bank%d" % t)[:] for t in range(PACK)]
                )
            for t in range(PACK):
                product(second_sums[half][t], t, z_codes[:], z_scales[:])

        for t in range(PACK):
            nc.scalar.activation(h_rows[t][:, HALVES[0]], second_sums[0][t], COPY, scale=0.0625)
        nc.scalar.activation(h_rows[0][:, HALVES[1]], second_sums[1][0], COPY, scale=0.0625)
        for t in range(1, PACK):
            nc.vector.tensor_scalar(h_rows[t][:, HALVES[1]], second_sums[1][t], 0.0625, None, MULT)

        bias3 = keep.tile([P, PACK], F32, align_bytes=64, tag="sg2_0")
        nc.vector.scalar_tensor_tensor(bias3[:], sl3_t[:], -1.0, th3_t[:], MULT, MULT)
        sg3 = keep.tile([P, PACK, S], F32, align_bytes=64, tag="sg_third")
        for t in range(PACK):
            col = slice(t, t + 1)
            nc.scalar.activation(
                sg3[:, t, :], h_rows[t][:].indirect(n3_list[:]), SIGMOID, bias=bias3[:, col], scale=sl3_t[:, col]
            )
            nc.vector.tensor_tensor(st_rows[t][:], h_rows[t][:, :S], sg3[:, t, :], MULT)

        out_rows = out_0.rearrange("(p t) c -> p t c", t=PACK)
        y_codes = keep.tile([P, S], I32, align_bytes=64)
        y_scales = keep.tile([P, S], U8, align_bytes=64)
        words_out = out_1[0].rearrange("p c r -> p (c r)").bitcast(I32)
        for half in range(2):
            cols, entries = HALVES[half], LIST_HALVES[half]
            result = keep.tile([P, PACK, HALF], F32, name="result%d" % half, align_bytes=64)
            for t in range(PACK):
                fetched = keep.tile([P, HALF], F32, name="fetched", align_bytes=64, bufs=4)
                nc.scalar.activation(fetched[:], st_rows[t][:].indirect(n4_list[:, entries]), COPY)
                nc.vector.scalar_tensor_tensor(result[:, t, :], fetched[:], -0.5, st_rows[t][:, cols], MULT, ADD)
            (nc.sync, nc.scalar)[half].dma_start(out_rows[:, :, cols], result[:])
            y = keep.tile([P, HALF * PACK], BF16, name="y%d" % half, align_bytes=64, tag="rounded")
            nc.vector.tensor_copy(interleaved(y), by_lines(result[:]))
            nc.vector.quantize_mx(out=y_codes[:, cols].bitcast(FP8X4), scales=y_scales[:, cols], in_=y[:])
            nc.sync.dma_start(words_out[:, cols], y_codes[:, cols])
        for q in range(4):
            queue = nc.scalar if q % 2 == 0 else nc.sync
            queue.dma_start(out_2[0, 4 * q : 4 * q + 4, :].bitcast(I32), y_scales[32 * q : 32 * q + 4, :].bitcast(I32))
